import numpy as np
import ml_dtypes


def mxq(x, axis, fmt="e4m3"):
    dtype, down = {"e4m3": (ml_dtypes.float8_e4m3fn, 7), "e5m2": (ml_dtypes.float8_e5m2, 14)}[fmt]
    v = np.moveaxis(np.asarray(x, np.float32).astype(ml_dtypes.bfloat16).astype(np.float64), axis, -1)
    blocks = v.reshape(v.shape[:-1] + (-1, 32))
    amax = np.abs(blocks).max(-1, keepdims=True)
    byte = np.maximum(np.where(amax > 0, np.frexp(amax)[1] - 1 + 127, 0) - down, 1)
    scale = np.exp2(byte - 127.0)
    codes = (blocks / scale).astype(np.float32).astype(dtype).astype(np.float64)
    return np.moveaxis((codes * scale).reshape(v.shape), -1, axis)


WIDE = False


def mx_kscale(k):
    if not WIDE:
        return np.ones(k)
    levels = np.array([10, -10, 5, -5, 0])
    if k % 512:
        return np.exp2(np.random.permutation(np.resize(levels, k // 32))).repeat(32)
    a = np.empty((k // 512, 16))
    for p in range(k // 512):
        a[p, :8] = np.random.permutation(np.resize(levels, 8))
        for g in range(8):
            far = levels[np.abs(levels - a[p, g]) >= 10]
            a[p, g + 8] = far[np.random.randint(len(far))]
    return np.exp2(a.ravel()).repeat(32)


def f64(x):
    return np.asarray(x).astype(np.float64)


def striped(idx):
    return np.tile(idx.reshape(-1, 16).T, (8, 1)).astype(np.uint16)


def unstriped(offs):
    return offs[:16].T.reshape(-1).astype(np.int64)


def striped8(idx):
    return np.concatenate([x.reshape(-1, 16).T for x in idx]).astype(np.uint16)


def runs(offs, k):
    lists = np.stack([offs[16 * r : 16 * r + 16].T.reshape(-1) for r in range(8)]).astype(np.int64)
    return lists[np.arange(k) % 512 // 64]


def pack_weight(w):
    k, n = w.shape
    w = f64(np.asarray(w, np.float32).astype(ml_dtypes.bfloat16)).reshape(k // 32, 32, n)
    amax = np.abs(w).max(1)
    byte = np.clip(np.where(amax > 0, np.frexp(amax)[1] - 1 + 127 - 7, 1), 1, 254)
    scaled = (w * np.exp2(127.0 - byte)[:, None, :]).reshape(k, n).astype(np.float32)
    words = np.ascontiguousarray(scaled.reshape(k // 512, 128, 4, n).transpose(0, 1, 3, 2)).astype(ml_dtypes.float8_e4m3fn).view(np.uint8)
    return words, np.ascontiguousarray(byte.astype(np.uint8).reshape(k // 512, 16, n))


def unpack_weight(words, scales):
    g, p, n, _ = words.shape
    vals = np.ascontiguousarray(words).view(ml_dtypes.float8_e4m3fn).astype(np.float64) * np.repeat(np.exp2(scales.astype(np.float64) - 127.0), 8, axis=1)[..., None]
    return vals.transpose(0, 1, 3, 2).reshape(g * 512, n)


def sigmoid(v):
    return 1.0 / (1.0 + np.exp(-np.maximum(v, -700.0)))


K, T, S, N, H, U = 512, 2048, 512, 512, 512, 1024


def setup_inputs():
    n = np.random.standard_normal
    s = mx_kscale(K)[:, None]
    u = mx_kscale(H)
    packed_xT = pack_weight(n((K, T)) * s)
    return {
        "x_words": packed_xT[0],
        "x_scales": packed_xT[1],
        "w1": (n((K, H)) / np.sqrt(K) / s).astype(np.float32),
        "w2": (n((K, H)) / np.sqrt(K) / s).astype(np.float32),
        "gn": (np.random.uniform(0.5, 1.5, (H, 1)) * u[:, None]).astype(np.float32),
        "w3": (n((H, N)) / np.sqrt(H) / u[:, None]).astype(np.float32),
        "mem": n((N, U)).astype(np.float32),
        "offs": striped(np.random.permutation(T)[:S]),
        "two": striped(np.random.permutation(T)[:S]),
        "t1": striped8(np.stack([np.random.permutation(S) for _ in range(8)])),
        "t2": striped8(np.stack([np.random.permutation(S) for _ in range(8)])),
        "t3": striped8(np.stack([np.random.permutation(S) for _ in range(8)])),
        "slot": striped8(np.stack([np.random.permutation(U)[:S] for _ in range(8)])),
    }


def reference(x_words, x_scales, w1, w2, gn, w3, mem, offs, two, t1, t2, t3, slot):
    x_two = unpack_weight(x_words, x_scales)[:, unstriped(two)]
    c = mxq(f64(w2), 0, "e4m3").T @ x_two
    xq = unpack_weight(x_words, x_scales)[:, unstriped(offs)]
    y = mxq(f64(w1), 0, "e4m3").T @ xq
    z = f64(gn) * (1.0 * (sigmoid(3.0 * (c - (y[np.arange(H)[:, None], runs(t1, H)]))) + sigmoid(3.0 * (c - (y[np.arange(H)[:, None], runs(t2, H)]))) + sigmoid(3.0 * (c - (y[np.arange(H)[:, None], runs(t3, H)])))) + -1.5)
    h = mxq(f64(w3), 0, "e4m3").T @ mxq(z, 0, "e4m3")
    out = f64(mem).copy()
    out[np.arange(N)[:, None], runs(slot, N)] = h
    return out

@@ -1,0 +1,251 @@
+from contextlib import ExitStack
+
+import concourse.mybir as mybir
+from concourse.masks import make_identity
+
+K, T, S, N, H, U = 512, 2048, 512, 512, 512, 1024
+FLOPS = 3 * 2 * 512 * 512 * 512
+
+F32 = mybir.dt.float32
+BF16 = mybir.dt.bfloat16
+I32 = mybir.dt.int32
+U32 = mybir.dt.uint32
+U16 = mybir.dt.uint16
+U8 = mybir.dt.uint8
+FP8X4 = mybir.dt.float8_e4m3fn_x4
+ACT = mybir.ActivationFunctionType
+ALU = mybir.AluOpType
+
+P = 128
+PACK = 4
+HALF = S // 2
+TAPS = 3
+
+
+def tile_picked_shadowpcf_none_p_kernel(
+    tc, x_words, x_scales, w1, w2, gn, w3, mem, offs, two, t1, t2, t3, slot, out
+):
+    nc = tc.nc
+    with ExitStack() as ctx:
+        keep = ctx.enter_context(tc.tile_pool(name="keep", bufs=1))
+        mm_ps = ctx.enter_context(tc.psum_pool(name="mm_ps", bufs=4))
+        tr_ps = ctx.enter_context(tc.psum_pool(name="tr_ps", bufs=2))
+        z_ps = ctx.enter_context(tc.psum_pool(name="z_ps", bufs=2))
+
+        def load_list(src, name):
+            tile = keep.tile([P, S // 16], U16, name=name)
+            nc.sync.dma_start(tile[:], src)
+            return tile
+
+        def load_weight_cols(w, name, part, parts):
+            width = H // parts
+            raw = keep.tile([P, PACK, width], F32, name=name)
+            nc.sync.dma_start(raw[:], w.rearrange("(p j) c -> p j c", j=PACK)[:, :, part * width : (part + 1) * width])
+            return raw
+
+        def cast_weight_cols(copy, grouped, raw, part, parts):
+            m = P // parts
+            dst = grouped[:].rearrange("p (t m j) -> p m j t", t=PACK, j=PACK)[:, part * m : (part + 1) * m]
+            copy(dst, raw[:].rearrange("p j (m t) -> p m j t", t=PACK))
+
+        def quantize(name, src, width):
+            codes = keep.tile([P, width], U32, name=name + "_codes", align_bytes=64)
+            scales = keep.tile([P, width], U8, name=name + "_scales", align_bytes=64)
+            nc.vector.quantize_mx(out=codes[:].bitcast(FP8X4), scales=scales[:], in_=src)
+            return codes, scales
+
+        def product(dst, stationary, moving, cols):
+            nc.tensor.matmul_mx(
+                out=dst,
+                lhsT=stationary[0].bitcast(FP8X4),
+                lhsT_scale=stationary[1],
+                rhs=moving[0][:, cols].bitcast(FP8X4),
+                rhs_scale=moving[1][:, cols],
+                start=True,
+                stop=True,
+            )
+
+        xs = keep.tile([P, T], U8, name="xs")
+        nc.gpsimd.memset(xs[:].bitcast(I32), 0)
+        for q in range(4):
+            nc.scalar.dma_start(xs[32 * q : 32 * q + 4, :].bitcast(I32), x_scales[0, 4 * q : 4 * q + 4, :].bitcast(I32))
+
+        offs_t = load_list(offs, "offs_t")
+        xw = keep.tile([P, T], U32, name="xw")
+        nc.sync.dma_start(xw[:].bitcast(I32), x_words[0].rearrange("p n r -> p (n r)").bitcast(I32))
+        two_t = load_list(two, "two_t")
+        w1_raw = [load_weight_cols(w1, "w1_raw%d" % i, i, 2) for i in range(2)]
+        w2_raw = [load_weight_cols(w2, "w2_raw%d" % i, i, 2) for i in range(2)]
+        taps = [load_list(src, name) for src, name in ((t1, "t1_t"), (t2, "t2_t"), (t3, "t3_t"))]
+        gain = keep.tile([P, PACK], F32, name="gain")
+        nc.sync.dma_start(gain[:], gn.rearrange("(p t) o -> p (t o)", t=PACK))
+        w3_raw = load_weight_cols(w3, "w3_raw", 0, 1)
+        slot_t = load_list(slot, "slot_t")
+        page = []
+        for t in range(PACK):
+            tile = keep.tile([P, U], F32, name="page%d" % t)
+            nc.sync.dma_start(tile[:], mem.rearrange("(p t) u -> p t u", t=PACK)[:, t, :])
+            page.append(tile)
+
+        ident = keep.tile([P, P], F32, name="ident")
+        make_identity(nc, ident[:])
+        half_gain = keep.tile([P, PACK], F32, name="half_gain")
+        nc.gpsimd.tensor_scalar(half_gain[:], gain[:], 0.5, 0.0, ALU.mult, ALU.add)
+        warm = keep.tile([P, 1], F32, name="warm")
+        nc.scalar.activation(warm[:], ident[:, 0:1], ACT.Tanh)
+
+        def pick(window, offsets, dtype, name):
+            tile = keep.tile([P, S], dtype, name=name, align_bytes=64)
+            nc.vector.tensor_copy(tile[:], window[:].indirect(offsets[:]))
+            return tile
+
+        w1_bf = keep.tile([P, PACK * H], BF16, name="w1_bf", align_bytes=64)
+        w2_bf = keep.tile([P, PACK * H], BF16, name="w2_bf", align_bytes=64)
+        w3_bf = keep.tile([P, PACK * H], BF16, name="w3_bf", align_bytes=64)
+        for i in range(2):
+            cast_weight_cols(nc.scalar.copy, w1_bf, w1_raw[i], i, 2)
+        xq_words = pick(xw, offs_t, U32, "xq_words")
+        xc_words = pick(xw, two_t, U32, "xc_words")
+        xq = (xq_words, pick(xs, offs_t, U8, "xq_scales"))
+        w1_q = quantize("w1", w1_bf[:], H)
+        xc = (xc_words, pick(xs, two_t, U8, "xc_scales"))
+        cast_weight_cols(nc.scalar.copy, w2_bf, w2_raw[0], 0, 2)
+        cast_weight_cols(nc.vector.tensor_copy, w2_bf, w2_raw[1], 1, 2)
+
+        def stationary(q, t):
+            return q[0][:, t * P : (t + 1) * P], q[1][:, t * P : (t + 1) * P]
+
+        y, c = [], {}
+
+        def project_y(t):
+            bank = mm_ps.tile([P, S], F32, name="bank", tag="bank")
+            product(bank[:], stationary(w1_q, t), xq, slice(0, S))
+            tile = keep.tile([P, S], F32, name="y%d" % t)
+            nc.scalar.copy(tile[:], bank[:])
+            y.append(tile)
+
+        w2_q = []
+
+        def project_c(half, t):
+            bank = mm_ps.tile([P, HALF], F32, name="bank", tag="bank")
+            product(bank[:], (w2_q[t][0][:], w2_q[t][1][:]), xc, slice(half * HALF, (half + 1) * HALF))
+            tile = keep.tile([P, HALF], F32, name="c%d_%d" % (half, t))
+            nc.scalar.copy(tile[:], bank[:])
+            c[half, t] = tile
+
+        lists_half = HALF // 16
+        z_bank = {}
+        diff = {}
+
+        def differences(half, t):
+            tag = "z_grouped0" if (half, t) == (1, 3) else "d%d_%d" % (half, t)
+            d = keep.tile([P, TAPS, HALF], F32, name="d", tag=tag, align_bytes=64)
+            for l in range(TAPS):
+                offsets = taps[l][:, half * lists_half : (half + 1) * lists_half]
+                nc.vector.tensor_tensor(d[:, l, :], y[t][:].indirect(offsets), c[half, t][:], ALU.subtract)
+            diff[half, t] = d
+
+        sum_bank = {}
+        late = []
+
+        def hide(half, t):
+            if (half, t) == (1, 1):
+                late.append(keep.tile([P, 2, TAPS, HALF], F32, name="late", tag="z_rows0"))
+            if half == 1 and t in (1, 2):
+                soft = late[0][:, t - 1]
+            else:
+                tag = "soft0_3" if (half, t) == (1, 0) else "soft%d_%d" % (half, t)
+                soft = keep.tile([P, TAPS, HALF], F32, name="soft", tag=tag)[:]
+            nc.scalar.activation(soft, diff[half, t][:], ACT.Tanh, scale=-1.5)
+            if t % 2 == 0:
+                sum_bank[half, t // 2] = tr_ps.tile([P, 2, 2, P], F32, name="turned", tag="turned")
+            bank = sum_bank[half, t // 2]
+            for b in range(2):
+                for l in range(TAPS):
+                    nc.tensor.matmul(bank[:, t % 2, b, :], soft[:, l, b * P : (b + 1) * P], ident[:], start=l == 0, stop=l == TAPS - 1, is_transpose=True)
+
+        def turn_back(half, pair):
+            sums = keep.tile([P, 2, 2, P], F32, name="sums%d_%d" % (half, pair))
+            nc.scalar.copy(sums[:], sum_bank[half, pair][:])
+            bank = z_ps.tile([P, 2, 2, P], F32, name="zbank", tag="zbank")
+            for tt in range(2):
+                for b in range(2):
+                    nc.tensor.transpose(bank[:, tt, b, :], sums[:, tt, b, :], ident[:])
+            z_bank[half, pair] = bank
+
+        z_rows = [keep.tile([P, PACK, HALF], BF16, name="z_rows", tag="z_rows%d" % h) for h in range(2)]
+        z_q = {}
+
+        def gain_out(half, pair):
+            for tt in range(2):
+                t = 2 * pair + tt
+                src = z_bank[half, pair][:, tt].rearrange("p b j -> p (b j)")
+                nc.scalar.activation(z_rows[half][:, t, :], src, ACT.Copy, scale=half_gain[:, t : t + 1])
+
+        def quantize_z(half):
+            grouped = keep.tile([P, HALF * PACK], BF16, name="z_grouped", tag="z_grouped%d" % half, align_bytes=64)
+            nc.scalar.copy(
+                grouped[:].rearrange("p (c i t) -> p c t i", i=4, t=PACK),
+                z_rows[half][:].rearrange("p t (c i) -> p c t i", i=4),
+            )
+            z_q[half] = quantize("z%d" % half, grouped[:], HALF)
+
+        h = {}
+        h_bank = {}
+
+        def layer(half, pair, pool, tag):
+            bank = pool.tile([P, 2, HALF], F32, name="hbank", tag=tag)
+            for tt in range(2):
+                product(bank[:, tt, :], stationary(w3_q, 2 * pair + tt), z_q[half], slice(0, HALF))
+            h_bank[half, pair] = bank
+
+        def layer_out(half, t):
+            tag = "z_rows1" if (half, t) == (0, 3) else "h%d_%d" % (half, t)
+            tile = keep.tile([P, HALF], F32, name="h", tag=tag)
+            nc.scalar.copy(tile[:], h_bank[half, t // 2][:, t % 2, :])
+            h[half, t] = tile
+
+        def put(half, t):
+            offsets = slot_t[:, half * lists_half : (half + 1) * lists_half]
+            nc.vector.tensor_copy(page[t][:].indirect(offsets), h[half, t][:])
+
+        project_y(0)
+        for t in range(PACK):
+            w2_q.append(quantize("w2_%d" % t, w2_bf[:, t * H : (t + 1) * H], P))
+            project_c(0, t)
+            if t + 1 < PACK:
+                project_y(t + 1)
+        for t in range(PACK):
+            differences(0, t)
+            project_c(1, t)
+            hide(0, t)
+            if t == 1:
+                cast_weight_cols(nc.scalar.copy, w3_bf, w3_raw, 0, 1)
+            if t % 2 == 1:
+                turn_back(0, t // 2)
+                gain_out(0, t // 2)
+        w3_q = quantize("w3", w3_bf[:], N)
+        quantize_z(0)
+        for pair in range(2):
+            layer(0, pair, mm_ps, "bank")
+        for t in range(PACK):
+            differences(1, t)
+            if t == 3:
+                for early in range(3):
+                    layer_out(0, early)
+            hide(1, t)
+            if t % 2 == 1:
+                turn_back(1, t // 2)
+                gain_out(1, t // 2)
+        for t in range(3):
+            put(0, t)
+        quantize_z(1)
+        layer_out(0, 3)
+        put(0, 3)
+        for pair in range(2):
+            layer(1, pair, mm_ps, "bank")
+        for t in range(PACK):
+            layer_out(1, t)
+        for t in range(PACK):
+            put(1, t)
+            nc.sync.dma_start(out.rearrange("(p t) u -> p t u", t=PACK)[:, t, :], page[t][:])

@@ -39,7 +39,7 @@ def tile_picked_shadowpcf_none_p_kernel(
 
         def load_weight_cols(w, name, part, parts):
             width = H // parts
-            raw = keep.tile([P, PACK, width], F32, name=name)
+            raw = keep.tile([P, PACK, width], F32, name="raw", tag=name, align_bytes=64)
             nc.sync.dma_start(raw[:], w.rearrange("(p j) c -> p j c", j=PACK)[:, :, part * width : (part + 1) * width])
             return raw
 
@@ -66,9 +66,9 @@ def tile_picked_shadowpcf_none_p_kernel(
             )
 
         xs = keep.tile([P, T], U8, name="xs")
-        nc.gpsimd.memset(xs[:].bitcast(I32), 0)
+        nc.vector.memset(xs[:].bitcast(I32), 0)
         for q in range(4):
-            nc.scalar.dma_start(xs[32 * q : 32 * q + 4, :].bitcast(I32), x_scales[0, 4 * q : 4 * q + 4, :].bitcast(I32))
+            nc.sync.dma_start(xs[32 * q : 32 * q + 4, :].bitcast(I32), x_scales[0, 4 * q : 4 * q + 4, :].bitcast(I32))
 
         offs_t = load_list(offs, "offs_t")
         xw = keep.tile([P, T], U32, name="xw")
@@ -79,7 +79,7 @@ def tile_picked_shadowpcf_none_p_kernel(
         taps = [load_list(src, name) for src, name in ((t1, "t1_t"), (t2, "t2_t"), (t3, "t3_t"))]
         gain = keep.tile([P, PACK], F32, name="gain")
         nc.sync.dma_start(gain[:], gn.rearrange("(p t) o -> p (t o)", t=PACK))
-        w3_raw = load_weight_cols(w3, "w3_raw", 0, 1)
+        w3_raw = [load_weight_cols(w3, "w3_raw%d" % i, i, 2) for i in range(2)]
         slot_t = load_list(slot, "slot_t")
         page = []
         for t in range(PACK):
@@ -94,21 +94,20 @@ def tile_picked_shadowpcf_none_p_kernel(
         warm = keep.tile([P, 1], F32, name="warm")
         nc.scalar.activation(warm[:], ident[:, 0:1], ACT.Tanh)
 
-        def pick(window, offsets, dtype, name):
-            tile = keep.tile([P, S], dtype, name=name, align_bytes=64)
-            nc.vector.tensor_copy(tile[:], window[:].indirect(offsets[:]))
+        def pick(window, offsets, dtype, tag):
+            tile = keep.tile([P, 16 * offsets.shape[1]], dtype, name="picked", tag=tag, align_bytes=64)
+            nc.vector.tensor_copy(tile[:], window[:].indirect(offsets))
             return tile
 
         w1_bf = keep.tile([P, PACK * H], BF16, name="w1_bf", align_bytes=64)
         w2_bf = keep.tile([P, PACK * H], BF16, name="w2_bf", align_bytes=64)
-        w3_bf = keep.tile([P, PACK * H], BF16, name="w3_bf", align_bytes=64)
         for i in range(2):
             cast_weight_cols(nc.scalar.copy, w1_bf, w1_raw[i], i, 2)
-        xq_words = pick(xw, offs_t, U32, "xq_words")
-        xc_words = pick(xw, two_t, U32, "xc_words")
-        xq = (xq_words, pick(xs, offs_t, U8, "xq_scales"))
+        xq_words = pick(xw, offs_t[:], U32, "xq_words")
+        xc_words = pick(xw, two_t[:, 0:16], U32, "xc_words")
+        xq = (xq_words, pick(xs, offs_t[:], U8, "xq_scales"))
         w1_q = quantize("w1", w1_bf[:], H)
-        xc = (xc_words, pick(xs, two_t, U8, "xc_scales"))
+        xc = [(xc_words, pick(xs, two_t[:, 0:16], U8, "xc_scales"))]
         cast_weight_cols(nc.scalar.copy, w2_bf, w2_raw[0], 0, 2)
         cast_weight_cols(nc.vector.tensor_copy, w2_bf, w2_raw[1], 1, 2)
 
@@ -128,7 +127,7 @@ def tile_picked_shadowpcf_none_p_kernel(
 
         def project_c(half, t):
             bank = mm_ps.tile([P, HALF], F32, name="bank", tag="bank")
-            product(bank[:], (w2_q[t][0][:], w2_q[t][1][:]), xc, slice(half * HALF, (half + 1) * HALF))
+            product(bank[:], (w2_q[t][0][:], w2_q[t][1][:]), xc[half], slice(0, HALF))
             tile = keep.tile([P, HALF], F32, name="c%d_%d" % (half, t))
             nc.scalar.copy(tile[:], bank[:])
             c[half, t] = tile
@@ -145,49 +144,43 @@ def tile_picked_shadowpcf_none_p_kernel(
                 nc.vector.tensor_tensor(d[:, l, :], y[t][:].indirect(offsets), c[half, t][:], ALU.subtract)
             diff[half, t] = d
 
-        sum_bank = {}
         late = []
+        sums = {}
 
         def hide(half, t):
-            if (half, t) == (1, 1):
-                late.append(keep.tile([P, 2, TAPS, HALF], F32, name="late", tag="z_rows0"))
-            if half == 1 and t in (1, 2):
-                soft = late[0][:, t - 1]
+            if (half, t) == (1, 0):
+                late.append(keep.tile([P, 3, TAPS, HALF], F32, name="late", tag="soft0_3"))
+            if half == 1 and t < 3:
+                soft = late[0][:, t]
             else:
-                tag = "soft0_3" if (half, t) == (1, 0) else "soft%d_%d" % (half, t)
-                soft = keep.tile([P, TAPS, HALF], F32, name="soft", tag=tag)[:]
-            nc.scalar.activation(soft, diff[half, t][:], ACT.Tanh, scale=-1.5)
-            if t % 2 == 0:
-                sum_bank[half, t // 2] = tr_ps.tile([P, 2, 2, P], F32, name="turned", tag="turned")
-            bank = sum_bank[half, t // 2]
+                soft = keep.tile([P, TAPS, HALF], F32, name="soft", tag="soft%d_%d" % (half, t))[:]
+            bank = tr_ps.tile([P, 2, P], F32, name="turned", tag="turned")
+            steps = [range(l, l + 1) for l in range(TAPS)] if t == PACK - 1 else [range(TAPS)]
+            for step in steps:
+                part = slice(step.start, step.stop)
+                nc.scalar.activation(soft[:, part], diff[half, t][:, part], ACT.Tanh, scale=-1.5)
+                for l in step:
+                    for b in range(2):
+                        first, last = (l, b) == (0, 0), (l, b) == (TAPS - 1, 1)
+                        nc.tensor.matmul(bank[:, b, :], soft[:, l, b * P : (b + 1) * P], ident[:], start=first, stop=last, is_transpose=True)
+            turned = keep.tile([P, 2, P], F32, name="sums", tag="sums%d_%d" % (half, t))
+            nc.scalar.copy(turned[:], bank[:])
             for b in range(2):
-                for l in range(TAPS):
-                    nc.tensor.matmul(bank[:, t % 2, b, :], soft[:, l, b * P : (b + 1) * P], ident[:], start=l == 0, stop=l == TAPS - 1, is_transpose=True)
+                if t == 0:
+                    z_bank[half, b] = z_ps.tile([P, PACK, P], F32, name="zbank", tag="zbank")
+                nc.tensor.transpose(z_bank[half, b][:, t, :], turned[:, b, :], ident[:])
 
-        def turn_back(half, pair):
-            sums = keep.tile([P, 2, 2, P], F32, name="sums%d_%d" % (half, pair))
-            nc.scalar.copy(sums[:], sum_bank[half, pair][:])
-            bank = z_ps.tile([P, 2, 2, P], F32, name="zbank", tag="zbank")
-            for tt in range(2):
-                for b in range(2):
-                    nc.tensor.transpose(bank[:, tt, b, :], sums[:, tt, b, :], ident[:])
-            z_bank[half, pair] = bank
-
-        z_rows = [keep.tile([P, PACK, HALF], BF16, name="z_rows", tag="z_rows%d" % h) for h in range(2)]
         z_q = {}
-
-        def gain_out(half, pair):
-            for tt in range(2):
-                t = 2 * pair + tt
-                src = z_bank[half, pair][:, tt].rearrange("p b j -> p (b j)")
-                nc.scalar.activation(z_rows[half][:, t, :], src, ACT.Copy, scale=half_gain[:, t : t + 1])
 
         def quantize_z(half):
             grouped = keep.tile([P, HALF * PACK], BF16, name="z_grouped", tag="z_grouped%d" % half, align_bytes=64)
-            nc.scalar.copy(
-                grouped[:].rearrange("p (c i t) -> p c t i", i=4, t=PACK),
-                z_rows[half][:].rearrange("p t (c i) -> p c t i", i=4),
-            )
+            for b in range(2):
+                nc.vector.tensor_tensor(
+                    grouped[:, b * P * PACK : (b + 1) * P * PACK].rearrange("p (j t) -> p j t", t=PACK),
+                    z_bank[half, b][:].rearrange("p t j -> p j t"),
+                    half_gain[:].unsqueeze(1).to_broadcast([P, P, PACK]),
+                    ALU.mult,
+                )
             z_q[half] = quantize("z%d" % half, grouped[:], HALF)
 
         h = {}
@@ -200,7 +193,7 @@ def tile_picked_shadowpcf_none_p_kernel(
             h_bank[half, pair] = bank
 
         def layer_out(half, t):
-            tag = "z_rows1" if (half, t) == (0, 3) else "h%d_%d" % (half, t)
+            tag = "sums1_3" if (half, t) == (0, 3) else "h%d_%d" % (half, t)
             tile = keep.tile([P, HALF], F32, name="h", tag=tag)
             nc.scalar.copy(tile[:], h_bank[half, t // 2][:, t % 2, :])
             h[half, t] = tile
@@ -215,15 +208,15 @@ def tile_picked_shadowpcf_none_p_kernel(
             project_c(0, t)
             if t + 1 < PACK:
                 project_y(t + 1)
+        xc.append((pick(xw, two_t[:, 16:32], U32, "w2_raw1"), pick(xs, two_t[:, 16:32], U8, "w2_raw0")))
         for t in range(PACK):
             differences(0, t)
             project_c(1, t)
             hide(0, t)
-            if t == 1:
-                cast_weight_cols(nc.scalar.copy, w3_bf, w3_raw, 0, 1)
-            if t % 2 == 1:
-                turn_back(0, t // 2)
-                gain_out(0, t // 2)
+            if t in (1, 2):
+                if t == 1:
+                    w3_bf = keep.tile([P, PACK * H], BF16, name="w3_bf", tag="d0_0", align_bytes=64)
+                cast_weight_cols(nc.scalar.copy, w3_bf, w3_raw[t - 1], t - 1, 2)
         w3_q = quantize("w3", w3_bf[:], N)
         quantize_z(0)
         for pair in range(2):
@@ -234,9 +227,6 @@ def tile_picked_shadowpcf_none_p_kernel(
                 for early in range(3):
                     layer_out(0, early)
             hide(1, t)
-            if t % 2 == 1:
-                turn_back(1, t // 2)
-                gain_out(1, t // 2)
         for t in range(3):
             put(0, t)
         quantize_z(1)

@@ -3,7 +3,7 @@ from contextlib import ExitStack
 import concourse.mybir as mybir
 from concourse.masks import make_identity
 
-K, T, S, N, H, U = 512, 2048, 512, 512, 512, 1024
+T, S, H, U = 2048, 512, 512, 1024
 FLOPS = 3 * 2 * 512 * 512 * 512
 
 F32 = mybir.dt.float32
@@ -18,8 +18,11 @@ ALU = mybir.AluOpType
 
 P = 128
 PACK = 4
-HALF = S // 2
+LAST = PACK - 1
 TAPS = 3
+HALF = S // 2
+HALF_COLS = HALF // 16
+BLOCKS = HALF // P
 
 
 def tile_picked_shadowpcf_none_p_kernel(
@@ -28,214 +31,211 @@ def tile_picked_shadowpcf_none_p_kernel(
     nc = tc.nc
     with ExitStack() as ctx:
         keep = ctx.enter_context(tc.tile_pool(name="keep", bufs=1))
-        mm_ps = ctx.enter_context(tc.psum_pool(name="mm_ps", bufs=4))
-        tr_ps = ctx.enter_context(tc.psum_pool(name="tr_ps", bufs=2))
-        z_ps = ctx.enter_context(tc.psum_pool(name="z_ps", bufs=2))
+        product_ps = ctx.enter_context(tc.psum_pool(name="product_ps", bufs=4))
+        turned_ps = ctx.enter_context(tc.psum_pool(name="turned_ps", bufs=2))
+        z_ps = ctx.enter_context(tc.psum_pool(name="z_ps", bufs=BLOCKS))
 
         def load_list(src, name):
             tile = keep.tile([P, S // 16], U16, name=name)
             nc.sync.dma_start(tile[:], src)
             return tile
 
-        def load_weight_cols(w, name, part, parts):
-            width = H // parts
-            raw = keep.tile([P, PACK, width], F32, name="raw", tag=name, align_bytes=64)
-            nc.sync.dma_start(raw[:], w.rearrange("(p j) c -> p j c", j=PACK)[:, :, part * width : (part + 1) * width])
-            return raw
+        def list_half(tile, half):
+            return tile[:, half * HALF_COLS : (half + 1) * HALF_COLS]
 
-        def cast_weight_cols(copy, grouped, raw, part, parts):
-            m = P // parts
-            dst = grouped[:].rearrange("p (t m j) -> p m j t", t=PACK, j=PACK)[:, part * m : (part + 1) * m]
-            copy(dst, raw[:].rearrange("p j (m t) -> p m j t", t=PACK))
+        def load_weight(w, name):
+            sides = []
+            for side in range(2):
+                raw = keep.tile([P, PACK, H // 2], F32, name="raw", tag="%s_raw%d" % (name, side), align_bytes=64)
+                cols = slice(side * H // 2, (side + 1) * H // 2)
+                nc.sync.dma_start(raw[:], w.rearrange("(p j) c -> p j c", j=PACK)[:, :, cols])
+                sides.append(raw)
+            return sides
+
+        def round_weight(copy, grouped, raw, side):
+            places = slice(side * P // 2, (side + 1) * P // 2)
+            dst = grouped[:].rearrange("p (t m j) -> p m t j", t=PACK, j=PACK)[:, places]
+            copy(dst, raw[side][:].rearrange("p j (m t) -> p m t j", t=PACK))
 
         def quantize(name, src, width):
-            codes = keep.tile([P, width], U32, name=name + "_codes", align_bytes=64)
+            words = keep.tile([P, width], U32, name=name + "_words", align_bytes=64)
             scales = keep.tile([P, width], U8, name=name + "_scales", align_bytes=64)
-            nc.vector.quantize_mx(out=codes[:].bitcast(FP8X4), scales=scales[:], in_=src)
-            return codes, scales
+            nc.vector.quantize_mx(out=words[:].bitcast(FP8X4), scales=scales[:], in_=src)
+            return words[:], scales[:]
 
-        def product(dst, stationary, moving, cols):
+        def row_tile(operand, t):
+            return operand[0][:, t * P : (t + 1) * P], operand[1][:, t * P : (t + 1) * P]
+
+        def product(dst, stationary, moving):
             nc.tensor.matmul_mx(
                 out=dst,
                 lhsT=stationary[0].bitcast(FP8X4),
                 lhsT_scale=stationary[1],
-                rhs=moving[0][:, cols].bitcast(FP8X4),
-                rhs_scale=moving[1][:, cols],
+                rhs=moving[0].bitcast(FP8X4),
+                rhs_scale=moving[1],
                 start=True,
                 stop=True,
             )
 
+        def pick(window, offsets, dtype, tag):
+            tile = keep.tile([P, 16 * offsets.shape[1]], dtype, name="picked", tag=tag, align_bytes=64)
+            nc.vector.tensor_copy(tile[:], window[:].indirect(offsets))
+            return tile[:]
+
         xs = keep.tile([P, T], U8, name="xs")
         nc.vector.memset(xs[:].bitcast(I32), 0)
-        for q in range(4):
+        for q in range(P // 32):
             nc.sync.dma_start(xs[32 * q : 32 * q + 4, :].bitcast(I32), x_scales[0, 4 * q : 4 * q + 4, :].bitcast(I32))
 
         offs_t = load_list(offs, "offs_t")
         xw = keep.tile([P, T], U32, name="xw")
         nc.sync.dma_start(xw[:].bitcast(I32), x_words[0].rearrange("p n r -> p (n r)").bitcast(I32))
         two_t = load_list(two, "two_t")
-        w1_raw = [load_weight_cols(w1, "w1_raw%d" % i, i, 2) for i in range(2)]
-        w2_raw = [load_weight_cols(w2, "w2_raw%d" % i, i, 2) for i in range(2)]
+        w1_raw = load_weight(w1, "w1")
+        w2_raw = load_weight(w2, "w2")
         taps = [load_list(src, name) for src, name in ((t1, "t1_t"), (t2, "t2_t"), (t3, "t3_t"))]
         gain = keep.tile([P, PACK], F32, name="gain")
         nc.sync.dma_start(gain[:], gn.rearrange("(p t) o -> p (t o)", t=PACK))
-        w3_raw = [load_weight_cols(w3, "w3_raw%d" % i, i, 2) for i in range(2)]
+        w3_raw = load_weight(w3, "w3")
         slot_t = load_list(slot, "slot_t")
         page = []
         for t in range(PACK):
-            tile = keep.tile([P, U], F32, name="page%d" % t)
-            nc.sync.dma_start(tile[:], mem.rearrange("(p t) u -> p t u", t=PACK)[:, t, :])
-            page.append(tile)
+            rows = keep.tile([P, U], F32, name="page%d" % t)
+            nc.sync.dma_start(rows[:], mem.rearrange("(p t) u -> p t u", t=PACK)[:, t, :])
+            page.append(rows)
 
         ident = keep.tile([P, P], F32, name="ident")
         make_identity(nc, ident[:])
-        half_gain = keep.tile([P, PACK], F32, name="half_gain")
+        half_gain = keep.tile([P, PACK], F32, name="half_gain", tag="half_gain")
         nc.gpsimd.tensor_scalar(half_gain[:], gain[:], 0.5, 0.0, ALU.mult, ALU.add)
+
         warm = keep.tile([P, 1], F32, name="warm")
         nc.scalar.activation(warm[:], ident[:, 0:1], ACT.Tanh)
 
-        def pick(window, offsets, dtype, tag):
-            tile = keep.tile([P, 16 * offsets.shape[1]], dtype, name="picked", tag=tag, align_bytes=64)
-            nc.vector.tensor_copy(tile[:], window[:].indirect(offsets))
-            return tile
-
         w1_bf = keep.tile([P, PACK * H], BF16, name="w1_bf", align_bytes=64)
         w2_bf = keep.tile([P, PACK * H], BF16, name="w2_bf", align_bytes=64)
-        for i in range(2):
-            cast_weight_cols(nc.scalar.copy, w1_bf, w1_raw[i], i, 2)
-        xq_words = pick(xw, offs_t[:], U32, "xq_words")
-        xc_words = pick(xw, two_t[:, 0:16], U32, "xc_words")
-        xq = (xq_words, pick(xs, offs_t[:], U8, "xq_scales"))
+        for side in range(2):
+            round_weight(nc.scalar.copy, w1_bf, w1_raw, side)
+        texel_words = pick(xw, offs_t[:], U32, "texel_words")
+        point_words = pick(xw, list_half(two_t, 0), U32, "point_words")
+        texels = (texel_words, pick(xs, offs_t[:], U8, "texel_scales"))
         w1_q = quantize("w1", w1_bf[:], H)
-        xc = [(xc_words, pick(xs, two_t[:, 0:16], U8, "xc_scales"))]
-        cast_weight_cols(nc.scalar.copy, w2_bf, w2_raw[0], 0, 2)
-        cast_weight_cols(nc.vector.tensor_copy, w2_bf, w2_raw[1], 1, 2)
+        points = [(point_words, pick(xs, list_half(two_t, 0), U8, "point_scales"))]
+        round_weight(nc.scalar.copy, w2_bf, w2_raw, 0)
+        round_weight(nc.vector.tensor_copy, w2_bf, w2_raw, 1)
 
-        def stationary(q, t):
-            return q[0][:, t * P : (t + 1) * P], q[1][:, t * P : (t + 1) * P]
-
-        y, c = [], {}
+        y, w2_q, c, diff, z_bank, z_q, h_bank, h = [], [], {}, {}, {}, {}, {}, {}
 
         def project_y(t):
-            bank = mm_ps.tile([P, S], F32, name="bank", tag="bank")
-            product(bank[:], stationary(w1_q, t), xq, slice(0, S))
-            tile = keep.tile([P, S], F32, name="y%d" % t)
-            nc.scalar.copy(tile[:], bank[:])
-            y.append(tile)
-
-        w2_q = []
+            bank = product_ps.tile([P, S], F32, name="bank", tag="bank")
+            product(bank[:], row_tile(w1_q, t), texels)
+            rows = keep.tile([P, S], F32, name="y%d" % t)
+            nc.scalar.copy(rows[:], bank[:])
+            y.append(rows)
 
         def project_c(half, t):
-            bank = mm_ps.tile([P, HALF], F32, name="bank", tag="bank")
-            product(bank[:], (w2_q[t][0][:], w2_q[t][1][:]), xc[half], slice(0, HALF))
-            tile = keep.tile([P, HALF], F32, name="c%d_%d" % (half, t))
-            nc.scalar.copy(tile[:], bank[:])
-            c[half, t] = tile
+            bank = product_ps.tile([P, HALF], F32, name="bank", tag="bank")
+            product(bank[:], w2_q[t], points[half])
+            rows = keep.tile([P, HALF], F32, name="c%d_%d" % (half, t))
+            nc.scalar.copy(rows[:], bank[:])
+            c[half, t] = rows
 
-        lists_half = HALF // 16
-        z_bank = {}
-        diff = {}
-
-        def differences(half, t):
-            tag = "z_grouped0" if (half, t) == (1, 3) else "d%d_%d" % (half, t)
+        def differences(half, t, tag):
             d = keep.tile([P, TAPS, HALF], F32, name="d", tag=tag, align_bytes=64)
-            for l in range(TAPS):
-                offsets = taps[l][:, half * lists_half : (half + 1) * lists_half]
-                nc.vector.tensor_tensor(d[:, l, :], y[t][:].indirect(offsets), c[half, t][:], ALU.subtract)
+            for tap in range(TAPS):
+                window = y[t][:].indirect(list_half(taps[tap], half))
+                nc.vector.tensor_tensor(d[:, tap, :], window, c[half, t][:], ALU.subtract)
             diff[half, t] = d
 
-        late = []
-        sums = {}
-
-        def hide(half, t):
-            if (half, t) == (1, 0):
-                late.append(keep.tile([P, 3, TAPS, HALF], F32, name="late", tag="soft0_3"))
-            if half == 1 and t < 3:
-                soft = late[0][:, t]
-            else:
-                soft = keep.tile([P, TAPS, HALF], F32, name="soft", tag="soft%d_%d" % (half, t))[:]
-            bank = tr_ps.tile([P, 2, P], F32, name="turned", tag="turned")
-            steps = [range(l, l + 1) for l in range(TAPS)] if t == PACK - 1 else [range(TAPS)]
+        def sum_taps(half, t, soft):
+            bank = turned_ps.tile([P, BLOCKS, P], F32, name="turned", tag="turned")
+            steps = [range(tap, tap + 1) for tap in range(TAPS)] if t == LAST else [range(TAPS)]
             for step in steps:
                 part = slice(step.start, step.stop)
                 nc.scalar.activation(soft[:, part], diff[half, t][:, part], ACT.Tanh, scale=-1.5)
-                for l in step:
-                    for b in range(2):
-                        first, last = (l, b) == (0, 0), (l, b) == (TAPS - 1, 1)
-                        nc.tensor.matmul(bank[:, b, :], soft[:, l, b * P : (b + 1) * P], ident[:], start=first, stop=last, is_transpose=True)
-            turned = keep.tile([P, 2, P], F32, name="sums", tag="sums%d_%d" % (half, t))
-            nc.scalar.copy(turned[:], bank[:])
-            for b in range(2):
+                for tap in step:
+                    for b in range(BLOCKS):
+                        nc.tensor.matmul(
+                            bank[:, b, :],
+                            soft[:, tap, b * P : (b + 1) * P],
+                            ident[:],
+                            start=(tap, b) == (0, 0),
+                            stop=(tap, b) == (TAPS - 1, BLOCKS - 1),
+                            is_transpose=True,
+                        )
+            sums = keep.tile([P, BLOCKS, P], F32, name="sums%d_%d" % (half, t))
+            nc.scalar.copy(sums[:], bank[:])
+            for b in range(BLOCKS):
                 if t == 0:
                     z_bank[half, b] = z_ps.tile([P, PACK, P], F32, name="zbank", tag="zbank")
-                nc.tensor.transpose(z_bank[half, b][:, t, :], turned[:, b, :], ident[:])
-
-        z_q = {}
+                nc.tensor.transpose(z_bank[half, b][:, t, :], sums[:, b, :], ident[:])
 
         def quantize_z(half):
             grouped = keep.tile([P, HALF * PACK], BF16, name="z_grouped", tag="z_grouped%d" % half, align_bytes=64)
-            for b in range(2):
+            for b in range(BLOCKS):
                 nc.vector.tensor_tensor(
-                    grouped[:, b * P * PACK : (b + 1) * P * PACK].rearrange("p (j t) -> p j t", t=PACK),
-                    z_bank[half, b][:].rearrange("p t j -> p j t"),
+                    grouped[:, b * P * PACK : (b + 1) * P * PACK].rearrange("p (e t) -> p e t", t=PACK),
+                    z_bank[half, b][:].rearrange("p t e -> p e t"),
                     half_gain[:].unsqueeze(1).to_broadcast([P, P, PACK]),
                     ALU.mult,
                 )
             z_q[half] = quantize("z%d" % half, grouped[:], HALF)
 
-        h = {}
-        h_bank = {}
+        def layer(half):
+            for pair in range(PACK // 2):
+                bank = product_ps.tile([P, 2, HALF], F32, name="hbank", tag="bank")
+                for side in range(2):
+                    product(bank[:, side, :], row_tile(w3_q, 2 * pair + side), z_q[half])
+                h_bank[half, pair] = bank
 
-        def layer(half, pair, pool, tag):
-            bank = pool.tile([P, 2, HALF], F32, name="hbank", tag=tag)
-            for tt in range(2):
-                product(bank[:, tt, :], stationary(w3_q, 2 * pair + tt), z_q[half], slice(0, HALF))
-            h_bank[half, pair] = bank
-
-        def layer_out(half, t):
-            tag = "sums1_3" if (half, t) == (0, 3) else "h%d_%d" % (half, t)
-            tile = keep.tile([P, HALF], F32, name="h", tag=tag)
-            nc.scalar.copy(tile[:], h_bank[half, t // 2][:, t % 2, :])
-            h[half, t] = tile
+        def layer_out(half, t, tag):
+            rows = keep.tile([P, HALF], F32, name="h", tag=tag)
+            nc.scalar.copy(rows[:], h_bank[half, t // 2][:, t % 2, :])
+            h[half, t] = rows
 
         def put(half, t):
-            offsets = slot_t[:, half * lists_half : (half + 1) * lists_half]
-            nc.vector.tensor_copy(page[t][:].indirect(offsets), h[half, t][:])
+            nc.vector.tensor_copy(page[t][:].indirect(list_half(slot_t, half)), h[half, t][:])
 
         project_y(0)
         for t in range(PACK):
             w2_q.append(quantize("w2_%d" % t, w2_bf[:, t * H : (t + 1) * H], P))
             project_c(0, t)
-            if t + 1 < PACK:
+            if t < LAST:
                 project_y(t + 1)
-        xc.append((pick(xw, two_t[:, 16:32], U32, "w2_raw1"), pick(xs, two_t[:, 16:32], U8, "w2_raw0")))
+
+        points.append((pick(xw, list_half(two_t, 1), U32, "w2_raw1"), pick(xs, list_half(two_t, 1), U8, "w2_raw0")))
+
         for t in range(PACK):
-            differences(0, t)
+            differences(0, t, "d0_%d" % t)
             project_c(1, t)
-            hide(0, t)
-            if t in (1, 2):
-                if t == 1:
-                    w3_bf = keep.tile([P, PACK * H], BF16, name="w3_bf", tag="d0_0", align_bytes=64)
-                cast_weight_cols(nc.scalar.copy, w3_bf, w3_raw[t - 1], t - 1, 2)
-        w3_q = quantize("w3", w3_bf[:], N)
+            soft = keep.tile([P, TAPS, HALF], F32, name="soft", tag="soft0_%d" % t)
+            sum_taps(0, t, soft[:])
+            if t == 1:
+                w3_bf = keep.tile([P, PACK * H], BF16, name="w3_bf", tag="d0_0", align_bytes=64)
+            if 0 < t < LAST:
+                round_weight(nc.scalar.copy, w3_bf, w3_raw, t - 1)
+        w3_q = quantize("w3", w3_bf[:], H)
         quantize_z(0)
-        for pair in range(2):
-            layer(0, pair, mm_ps, "bank")
-        for t in range(PACK):
-            differences(1, t)
-            if t == 3:
-                for early in range(3):
-                    layer_out(0, early)
-            hide(1, t)
-        for t in range(3):
+        layer(0)
+
+        later = keep.tile([P, LAST, TAPS, HALF], F32, name="later", tag="soft0_%d" % LAST)
+        for t in range(LAST):
+            differences(1, t, "d1_%d" % t)
+            sum_taps(1, t, later[:, t])
+        differences(1, LAST, "z_grouped0")
+        for t in range(LAST):
+            layer_out(0, t, "h0_%d" % t)
+        soft = keep.tile([P, TAPS, HALF], F32, name="soft", tag="soft1_%d" % LAST)
+        sum_taps(1, LAST, soft[:])
+
+        for t in range(LAST):
             put(0, t)
         quantize_z(1)
-        layer_out(0, 3)
-        put(0, 3)
-        for pair in range(2):
-            layer(1, pair, mm_ps, "bank")
+        layer_out(0, LAST, "half_gain")
+        put(0, LAST)
+        layer(1)
         for t in range(PACK):
-            layer_out(1, t)
+            layer_out(1, t, "h1_%d" % t)
         for t in range(PACK):
             put(1, t)
             nc.sync.dma_start(out.rearrange("(p t) u -> p t u", t=PACK)[:, t, :], page[t][:])

from contextlib import ExitStack

import concourse.mybir as mybir
from concourse.masks import make_identity

T, S, H, U = 2048, 512, 512, 1024
FLOPS = 3 * 2 * 512 * 512 * 512

F32 = mybir.dt.float32
BF16 = mybir.dt.bfloat16
I32 = mybir.dt.int32
U32 = mybir.dt.uint32
U16 = mybir.dt.uint16
U8 = mybir.dt.uint8
FP8X4 = mybir.dt.float8_e4m3fn_x4
ACT = mybir.ActivationFunctionType
ALU = mybir.AluOpType

P = 128
PACK = 4
LAST = PACK - 1
TAPS = 3
HALF = S // 2
HALF_COLS = HALF // 16
BLOCKS = HALF // P


def tile_picked_shadowpcf_none_p_kernel(
    tc, x_words, x_scales, w1, w2, gn, w3, mem, offs, two, t1, t2, t3, slot, out
):
    nc = tc.nc
    with ExitStack() as ctx:
        keep = ctx.enter_context(tc.tile_pool(name="keep", bufs=1))
        product_ps = ctx.enter_context(tc.psum_pool(name="product_ps", bufs=4))
        turned_ps = ctx.enter_context(tc.psum_pool(name="turned_ps", bufs=2))
        z_ps = ctx.enter_context(tc.psum_pool(name="z_ps", bufs=BLOCKS))

        def load_list(src, name):
            tile = keep.tile([P, S // 16], U16, name=name)
            nc.sync.dma_start(tile[:], src)
            return tile

        def list_half(tile, half):
            return tile[:, half * HALF_COLS : (half + 1) * HALF_COLS]

        def load_weight(w, name):
            sides = []
            for side in range(2):
                raw = keep.tile([P, PACK, H // 2], F32, name="raw", tag="%s_raw%d" % (name, side), align_bytes=64)
                cols = slice(side * H // 2, (side + 1) * H // 2)
                nc.sync.dma_start(raw[:], w.rearrange("(p j) c -> p j c", j=PACK)[:, :, cols])
                sides.append(raw)
            return sides

        def round_weight(copy, grouped, raw, side):
            places = slice(side * P // 2, (side + 1) * P // 2)
            dst = grouped[:].rearrange("p (t m j) -> p m t j", t=PACK, j=PACK)[:, places]
            copy(dst, raw[side][:].rearrange("p j (m t) -> p m t j", t=PACK))

        def quantize(name, src, width):
            words = keep.tile([P, width], U32, name=name + "_words", align_bytes=64)
            scales = keep.tile([P, width], U8, name=name + "_scales", align_bytes=64)
            nc.vector.quantize_mx(out=words[:].bitcast(FP8X4), scales=scales[:], in_=src)
            return words[:], scales[:]

        def row_tile(operand, t):
            return operand[0][:, t * P : (t + 1) * P], operand[1][:, t * P : (t + 1) * P]

        def product(dst, stationary, moving):
            nc.tensor.matmul_mx(
                out=dst,
                lhsT=stationary[0].bitcast(FP8X4),
                lhsT_scale=stationary[1],
                rhs=moving[0].bitcast(FP8X4),
                rhs_scale=moving[1],
                start=True,
                stop=True,
            )

        def pick(window, offsets, dtype, tag):
            tile = keep.tile([P, 16 * offsets.shape[1]], dtype, name="picked", tag=tag, align_bytes=64)
            nc.vector.tensor_copy(tile[:], window[:].indirect(offsets))
            return tile[:]

        xs = keep.tile([P, T], U8, name="xs")
        nc.vector.memset(xs[:].bitcast(I32), 0)
        for q in range(P // 32):
            nc.sync.dma_start(xs[32 * q : 32 * q + 4, :].bitcast(I32), x_scales[0, 4 * q : 4 * q + 4, :].bitcast(I32))

        offs_t = load_list(offs, "offs_t")
        xw = keep.tile([P, T], U32, name="xw")
        nc.sync.dma_start(xw[:].bitcast(I32), x_words[0].rearrange("p n r -> p (n r)").bitcast(I32))
        two_t = load_list(two, "two_t")
        w1_raw = load_weight(w1, "w1")
        w2_raw = load_weight(w2, "w2")
        taps = [load_list(src, name) for src, name in ((t1, "t1_t"), (t2, "t2_t"), (t3, "t3_t"))]
        gain = keep.tile([P, PACK], F32, name="gain")
        nc.sync.dma_start(gain[:], gn.rearrange("(p t) o -> p (t o)", t=PACK))
        w3_raw = load_weight(w3, "w3")
        slot_t = load_list(slot, "slot_t")
        page = []
        for t in range(PACK):
            rows = keep.tile([P, U], F32, name="page%d" % t)
            nc.sync.dma_start(rows[:], mem.rearrange("(p t) u -> p t u", t=PACK)[:, t, :])
            page.append(rows)

        ident = keep.tile([P, P], F32, name="ident")
        make_identity(nc, ident[:])
        half_gain = keep.tile([P, PACK], F32, name="half_gain", tag="half_gain")
        nc.gpsimd.tensor_scalar(half_gain[:], gain[:], 0.5, 0.0, ALU.mult, ALU.add)

        warm = keep.tile([P, 1], F32, name="warm")
        nc.scalar.activation(warm[:], ident[:, 0:1], ACT.Tanh)

        w1_bf = keep.tile([P, PACK * H], BF16, name="w1_bf", align_bytes=64)
        w2_bf = keep.tile([P, PACK * H], BF16, name="w2_bf", align_bytes=64)
        for side in range(2):
            round_weight(nc.scalar.copy, w1_bf, w1_raw, side)
        texel_words = pick(xw, offs_t[:], U32, "texel_words")
        point_words = pick(xw, list_half(two_t, 0), U32, "point_words")
        texels = (texel_words, pick(xs, offs_t[:], U8, "texel_scales"))
        w1_q = quantize("w1", w1_bf[:], H)
        points = [(point_words, pick(xs, list_half(two_t, 0), U8, "point_scales"))]
        round_weight(nc.scalar.copy, w2_bf, w2_raw, 0)
        round_weight(nc.vector.tensor_copy, w2_bf, w2_raw, 1)

        y, w2_q, c, diff, z_bank, z_q, h_bank, h = [], [], {}, {}, {}, {}, {}, {}

        def project_y(t):
            bank = product_ps.tile([P, S], F32, name="bank", tag="bank")
            product(bank[:], row_tile(w1_q, t), texels)
            rows = keep.tile([P, S], F32, name="y%d" % t)
            nc.scalar.copy(rows[:], bank[:])
            y.append(rows)

        def project_c(half, t):
            bank = product_ps.tile([P, HALF], F32, name="bank", tag="bank")
            product(bank[:], w2_q[t], points[half])
            rows = keep.tile([P, HALF], F32, name="c%d_%d" % (half, t))
            nc.scalar.copy(rows[:], bank[:])
            c[half, t] = rows

        def differences(half, t, tag):
            d = keep.tile([P, TAPS, HALF], F32, name="d", tag=tag, align_bytes=64)
            for tap in range(TAPS):
                window = y[t][:].indirect(list_half(taps[tap], half))
                nc.vector.tensor_tensor(d[:, tap, :], window, c[half, t][:], ALU.subtract)
            diff[half, t] = d

        def sum_taps(half, t, soft):
            bank = turned_ps.tile([P, BLOCKS, P], F32, name="turned", tag="turned")
            steps = [range(tap, tap + 1) for tap in range(TAPS)] if t == LAST else [range(TAPS)]
            for step in steps:
                part = slice(step.start, step.stop)
                nc.scalar.activation(soft[:, part], diff[half, t][:, part], ACT.Tanh, scale=-1.5)
                for tap in step:
                    for b in range(BLOCKS):
                        nc.tensor.matmul(
                            bank[:, b, :],
                            soft[:, tap, b * P : (b + 1) * P],
                            ident[:],
                            start=(tap, b) == (0, 0),
                            stop=(tap, b) == (TAPS - 1, BLOCKS - 1),
                            is_transpose=True,
                        )
            sums = keep.tile([P, BLOCKS, P], F32, name="sums%d_%d" % (half, t))
            nc.scalar.copy(sums[:], bank[:])
            for b in range(BLOCKS):
                if t == 0:
                    z_bank[half, b] = z_ps.tile([P, PACK, P], F32, name="zbank", tag="zbank")
                nc.tensor.transpose(z_bank[half, b][:, t, :], sums[:, b, :], ident[:])

        def quantize_z(half):
            grouped = keep.tile([P, HALF * PACK], BF16, name="z_grouped", tag="z_grouped%d" % half, align_bytes=64)
            for b in range(BLOCKS):
                nc.vector.tensor_tensor(
                    grouped[:, b * P * PACK : (b + 1) * P * PACK].rearrange("p (e t) -> p e t", t=PACK),
                    z_bank[half, b][:].rearrange("p t e -> p e t"),
                    half_gain[:].unsqueeze(1).to_broadcast([P, P, PACK]),
                    ALU.mult,
                )
            z_q[half] = quantize("z%d" % half, grouped[:], HALF)

        def layer(half):
            for pair in range(PACK // 2):
                bank = product_ps.tile([P, 2, HALF], F32, name="hbank", tag="bank")
                for side in range(2):
                    product(bank[:, side, :], row_tile(w3_q, 2 * pair + side), z_q[half])
                h_bank[half, pair] = bank

        def layer_out(half, t, tag):
            rows = keep.tile([P, HALF], F32, name="h", tag=tag)
            nc.scalar.copy(rows[:], h_bank[half, t // 2][:, t % 2, :])
            h[half, t] = rows

        def put(half, t):
            nc.vector.tensor_copy(page[t][:].indirect(list_half(slot_t, half)), h[half, t][:])

        project_y(0)
        for t in range(PACK):
            w2_q.append(quantize("w2_%d" % t, w2_bf[:, t * H : (t + 1) * H], P))
            project_c(0, t)
            if t < LAST:
                project_y(t + 1)

        points.append((pick(xw, list_half(two_t, 1), U32, "w2_raw1"), pick(xs, list_half(two_t, 1), U8, "w2_raw0")))

        for t in range(PACK):
            differences(0, t, "d0_%d" % t)
            project_c(1, t)
            soft = keep.tile([P, TAPS, HALF], F32, name="soft", tag="soft0_%d" % t)
            sum_taps(0, t, soft[:])
            if t == 1:
                w3_bf = keep.tile([P, PACK * H], BF16, name="w3_bf", tag="d0_0", align_bytes=64)
            if 0 < t < LAST:
                round_weight(nc.scalar.copy, w3_bf, w3_raw, t - 1)
        w3_q = quantize("w3", w3_bf[:], H)
        quantize_z(0)
        layer(0)

        later = keep.tile([P, LAST, TAPS, HALF], F32, name="later", tag="soft0_%d" % LAST)
        for t in range(LAST):
            differences(1, t, "d1_%d" % t)
            sum_taps(1, t, later[:, t])
        differences(1, LAST, "z_grouped0")
        for t in range(LAST):
            layer_out(0, t, "h0_%d" % t)
        soft = keep.tile([P, TAPS, HALF], F32, name="soft", tag="soft1_%d" % LAST)
        sum_taps(1, LAST, soft[:])

        for t in range(LAST):
            put(0, t)
        quantize_z(1)
        layer_out(0, LAST, "half_gain")
        put(0, LAST)
        layer(1)
        for t in range(PACK):
            layer_out(1, t, "h1_%d" % t)
        for t in range(PACK):
            put(1, t)
            nc.sync.dma_start(out.rearrange("(p t) u -> p t u", t=PACK)[:, t, :], page[t][:])
